import numpy as np
CORES = [125,109,93,77,61,45,29,13,114,98,82,66,50,34,18,2]
N = 16
def setup_inputs(rng):
    return {"x": rng.standard_normal((N, 128, 128), dtype=np.float32)}
def reference(x):
    g = np.concatenate(list(x), axis=1)
    return {"y": np.broadcast_to(g, (N,) + g.shape)}

@@ -1,0 +1,147 @@
+from concourse.bass import DstId, RemoteDMATransfer
+
+NS, G, W, Q = 9, 3, 3, 4
+SCRATCH = {
+    "buf": ("dram", [NS, 128, 32], "float32"),
+}
+SEMAPHORES = ["xld", "xl", "xs", "own", "loc",
+              "h0", "h1", "h2", "c0", "c1", "c2", "r0", "r1", "r2", "s0", "s1", "s2"]
+FC = (3, 6)
+STAGE = 7
+NITEMS = 20
+
+
+def rcore(ch):
+    return 8 * ch + (2 if ch % 2 == 0 else 5)
+
+
+def helper_list(ch):
+    r = rcore(ch) % 8
+    return [8 * ch + k for k in range(8) if k != r and k not in FC] + [8 * ch + k for k in FC]
+
+
+def block_order(d):
+    return ([(d - 2) % 16, d ^ 1] + [(d - 2 * e) % 16 for e in range(2, 8)]
+            + [((d ^ 1) - 2 * e) % 16 for e in range(1, 8)])
+
+
+def landing(d, b, t):
+    k, j = divmod(4 * b + t, G)
+    if k == 0:
+        return rcore(d), 6 + j, -1
+    return helper_list(d)[(k - 1) % 7], G * ((k - 1) // 7) + j, (k - 1) // 7
+
+
+def did(topo, c):
+    rid, pid, _ = topo.addr(c)
+    return DstId(rid=rid, pnc=pid)
+
+
+def rank_core(g, core, T, topo):
+    ch = core // 8
+    sem, buf = T.sem, T.buf
+    me = T.rank_of(core)
+    g.sync.dma_start(buf[0:Q], T.x[:, :]).then_inc(sem.xld, 16)
+    g.wait_ge(sem.xld, 16)
+    trs = []
+    for t in range(Q):
+        trs.append(RemoteDMATransfer(dst_ids=[did(topo, 8 * ch + FC[t // 2])], dma_engine_mask=0x3 << (8 + 2 * t),
+                                     remote_sem=sem.xs, src=buf[t], dst=buf[STAGE + t % 2]))
+    nxt = rcore((ch + 2) % 16)
+    for t in range(G):
+        trs.append(RemoteDMATransfer(dst_ids=[did(topo, nxt)], dma_engine_mask=0x3 << (2 * t),
+                                     remote_sem=sem.r2, src=buf[t], dst=buf[6 + t]))
+    g.remote_dma_fused(trs, local_sem=sem.xl)
+    left = 2 * len(trs)
+    g.scalar.wait_ge(sem.xl, left)
+    g.scalar.dma_start(T.y[:, 128 * me:128 * me + 128], T.x[:, :]).then_inc(sem.own, 16)
+
+    order = block_order(ch)
+    units = [(s, t) for s in order for t in range(Q)]
+    hl = helper_list(ch)
+    ncred = [0]
+
+    def credit(k):
+        rid, pid, _ = topo.addr(hl[(k - 1) % 7])
+        g.remote_sem_update(remote_sem=sem["c%d" % ((k - 1) // 7)], local_sem=sem.loc, pid=pid, routing_id=rid,
+                            dma_engine_mask=1)
+        ncred[0] += 1
+
+    g.wait_ge(sem.xl, left)
+    credit(1)
+    credit(2)
+    arrived = [0] * W
+    stored = [0] * W
+    queues = (g.sync, g.scalar)
+    for k in range(NITEMS):
+        grp = (k + 2) % W
+        arrived[grp] += 6 if k == 0 else 12
+        item = units[G * k:G * k + G]
+        runs = []
+        for j, (s, t) in enumerate(item):
+            if runs and runs[-1][0] == s:
+                runs[-1][3] += 1
+            else:
+                runs.append([s, t, G * grp + j, 1])
+        for r, (s, t, slot, n) in enumerate(runs):
+            q = queues[(k + r) % 2]
+            col = 128 * T.rank_of(rcore(s))
+            q.wait_ge(sem["r%d" % grp], arrived[grp])
+            q.dma_start(T.y[32 * t:32 * (t + n), col:col + 128],
+                        buf[slot:slot + n]).then_inc(sem["s%d" % grp], 16)
+            stored[grp] += 16
+        g.wait_ge(sem["s%d" % grp], stored[grp])
+        if k + W < NITEMS:
+            credit(k + W)
+    g.wait_ge(sem.own, 16)
+    g.wait_ge(sem.loc, ncred[0])
+
+
+def helper_core(g, core, T, topo):
+    ch = core // 8
+    sem, buf = T.sem, T.buf
+    hl = helper_list(ch)
+    pos = hl.index(core)
+    loc = 0
+    if core % 8 in FC:
+        f = FC.index(core % 8)
+        g.wait_ge(sem.xs, 4)
+        for i in range(3):
+            trs = []
+            for u in range(2):
+                t = 2 * f + u
+                dst = []
+                for d in range(16):
+                    if d == ch:
+                        continue
+                    b = block_order(d).index(ch)
+                    c, slot, idx = landing(d, b, t)
+                    if idx == i:
+                        dst.append((b, c, slot))
+                dst.sort()
+                if dst:
+                    trs.append(RemoteDMATransfer(dst_ids=[did(topo, c) for _, c, _ in dst],
+                                                 dma_engine_mask=0xF << (4 * u), remote_sem=sem["h%d" % i],
+                                                 srcs=[buf[STAGE + u]], dsts=[buf[slot] for _, _, slot in dst]))
+            g.remote_dma_fused(trs, local_sem=sem.loc)
+            loc += 4 * len(trs)
+    r = did(topo, rcore(ch))
+    for i in range(3):
+        k = 1 + pos + 7 * i
+        if k >= NITEMS:
+            break
+        grp = (k + 2) % W
+        g.wait_ge(sem["h%d" % i], 12)
+        g.wait_ge(sem["c%d" % i], 1)
+        trs = [RemoteDMATransfer(dst_ids=[r], dma_engine_mask=0xF << (4 * j), remote_sem=sem["r%d" % grp],
+                                 src=buf[G * i + j], dst=buf[G * grp + j]) for j in range(G)]
+        g.remote_dma_fused(trs, local_sem=sem.loc)
+        loc += 12
+    g.wait_ge(sem.loc, loc)
+
+
+def rank_program(g, core, T, topo):
+    if core == rcore(core // 8):
+        rank_core(g, core, T, topo)
+    else:
+        helper_core(g, core, T, topo)

@@ -1,14 +1,17 @@
 from concourse.bass import DstId, RemoteDMATransfer
 
-NS, G, W, Q = 9, 3, 3, 4
+NS, Q = 9, 4
+GROUPS = ((0, 2), (2, 2), (4, 2), (6, 2), (8, 1))
+W = len(GROUPS)
+NC = 6
+ENG = {1: 16, 2: 8, 3: 4, 4: 4, 5: 2}
 SCRATCH = {
     "buf": ("dram", [NS, 128, 32], "float32"),
 }
-SEMAPHORES = ["xld", "xl", "xs", "own", "loc",
-              "h0", "h1", "h2", "c0", "c1", "c2", "r0", "r1", "r2", "s0", "s1", "s2"]
+SEMAPHORES = (["xld", "xl", "xs", "own", "loc", "h0", "h1", "h2"] + ["c%d" % i for i in range(NC)]
+              + ["r%d" % i for i in range(W)] + ["s%d" % i for i in range(W)])
 FC = (3, 6)
 STAGE = 7
-NITEMS = 20
 
 
 def rcore(ch):
@@ -25,11 +28,40 @@ def block_order(d):
             + [((d ^ 1) - 2 * e) % 16 for e in range(1, 8)])
 
 
-def landing(d, b, t):
-    k, j = divmod(4 * b + t, G)
-    if k == 0:
-        return rcore(d), 6 + j, -1
-    return helper_list(d)[(k - 1) % 7], G * ((k - 1) // 7) + j, (k - 1) // 7
+def make_plan():
+    units = [(b, t) for b in range(15) for t in range(Q)]
+    items, nxt, virgin, ptr = [], [], [], 0
+    for gi, (s0, n) in enumerate(GROUPS):
+        if s0 >= Q and ptr < Q:
+            take = min(n, Q - ptr)
+            items.append({"grp": gi, "units": units[ptr:ptr + take], "pos": -1, "credit": False})
+            ptr += take
+            nxt.append(5)
+            virgin.append(False)
+        else:
+            nxt.append(4)
+            virgin.append(s0 >= Q)
+    free = [NS] * 5 + [STAGE] * 2
+    used = [0] * 7
+    count = [0] * 7
+    last = [p - 7 for p in range(7)]
+    while ptr < len(units):
+        gi = min(range(W), key=lambda i: (nxt[i], i))
+        take = min(GROUPS[gi][1], len(units) - ptr)
+        p = min([p for p in range(7) if free[p] - used[p] >= take],
+                key=lambda p: ((free[p] - used[p] - take) % 2 if take == 1 else 0, last[p]))
+        items.append({"grp": gi, "units": units[ptr:ptr + take], "pos": p, "credit": not virgin[gi],
+                      "n": count[p], "slot": used[p]})
+        virgin[gi] = False
+        last[p] = len(items)
+        used[p] += take
+        count[p] += 1
+        ptr += take
+        nxt[gi] += 3
+    return items
+
+
+PLAN = make_plan()
 
 
 def did(topo, c):
@@ -47,52 +79,61 @@ def rank_core(g, core, T, topo):
     for t in range(Q):
         trs.append(RemoteDMATransfer(dst_ids=[did(topo, 8 * ch + FC[t // 2])], dma_engine_mask=0x3 << (8 + 2 * t),
                                      remote_sem=sem.xs, src=buf[t], dst=buf[STAGE + t % 2]))
-    nxt = rcore((ch + 2) % 16)
-    for t in range(G):
-        trs.append(RemoteDMATransfer(dst_ids=[did(topo, nxt)], dma_engine_mask=0x3 << (2 * t),
-                                     remote_sem=sem.r2, src=buf[t], dst=buf[6 + t]))
+    nxt = did(topo, rcore((ch + 2) % 16))
+    for it in PLAN:
+        if it["pos"] < 0:
+            for j, (b, t) in enumerate(it["units"]):
+                trs.append(RemoteDMATransfer(dst_ids=[nxt], dma_engine_mask=0x3 << (2 * t),
+                                             remote_sem=sem["r%d" % it["grp"]], src=buf[t],
+                                             dst=buf[GROUPS[it["grp"]][0] + j]))
     g.remote_dma_fused(trs, local_sem=sem.xl)
     left = 2 * len(trs)
     g.scalar.wait_ge(sem.xl, left)
     g.scalar.dma_start(T.y[:, 128 * me:128 * me + 128], T.x[:, :]).then_inc(sem.own, 16)
 
     order = block_order(ch)
-    units = [(s, t) for s in order for t in range(Q)]
     hl = helper_list(ch)
     ncred = [0]
 
-    def credit(k):
-        rid, pid, _ = topo.addr(hl[(k - 1) % 7])
-        g.remote_sem_update(remote_sem=sem["c%d" % ((k - 1) // 7)], local_sem=sem.loc, pid=pid, routing_id=rid,
+    def credit(it):
+        rid, pid, _ = topo.addr(hl[it["pos"]])
+        g.remote_sem_update(remote_sem=sem["c%d" % it["n"]], local_sem=sem.loc, pid=pid, routing_id=rid,
                             dma_engine_mask=1)
         ncred[0] += 1
 
     g.wait_ge(sem.xl, left)
-    credit(1)
-    credit(2)
+    seen = set()
+    for it in PLAN:
+        if it["grp"] not in seen and it["credit"]:
+            credit(it)
+        seen.add(it["grp"])
     arrived = [0] * W
     stored = [0] * W
     queues = (g.sync, g.scalar)
-    for k in range(NITEMS):
-        grp = (k + 2) % W
-        arrived[grp] += 6 if k == 0 else 12
-        item = units[G * k:G * k + G]
+    nq = 0
+    for k, it in enumerate(PLAN):
+        grp = it["grp"]
+        n = len(it["units"])
+        arrived[grp] += n * (2 if it["pos"] < 0 else ENG[n])
         runs = []
-        for j, (s, t) in enumerate(item):
-            if runs and runs[-1][0] == s:
+        for j, (b, t) in enumerate(it["units"]):
+            if runs and runs[-1][0] == b:
                 runs[-1][3] += 1
             else:
-                runs.append([s, t, G * grp + j, 1])
-        for r, (s, t, slot, n) in enumerate(runs):
-            q = queues[(k + r) % 2]
-            col = 128 * T.rank_of(rcore(s))
+                runs.append([b, t, GROUPS[grp][0] + j, 1])
+        for b, t, slot, m in runs:
+            q = queues[nq % 2]
+            nq += 1
+            col = 128 * T.rank_of(rcore(order[b]))
             q.wait_ge(sem["r%d" % grp], arrived[grp])
-            q.dma_start(T.y[32 * t:32 * (t + n), col:col + 128],
-                        buf[slot:slot + n]).then_inc(sem["s%d" % grp], 16)
+            q.dma_start(T.y[32 * t:32 * (t + m), col:col + 128],
+                        buf[slot:slot + m]).then_inc(sem["s%d" % grp], 16)
             stored[grp] += 16
         g.wait_ge(sem["s%d" % grp], stored[grp])
-        if k + W < NITEMS:
-            credit(k + W)
+        for later in PLAN[k + 1:]:
+            if later["grp"] == grp:
+                credit(later)
+                break
     g.wait_ge(sem.own, 16)
     g.wait_ge(sem.loc, ncred[0])
 
@@ -100,8 +141,7 @@ def rank_core(g, core, T, topo):
 def helper_core(g, core, T, topo):
     ch = core // 8
     sem, buf = T.sem, T.buf
-    hl = helper_list(ch)
-    pos = hl.index(core)
+    pos = helper_list(ch).index(core)
     loc = 0
     if core % 8 in FC:
         f = FC.index(core % 8)
@@ -109,15 +149,14 @@ def helper_core(g, core, T, topo):
         for i in range(3):
             trs = []
             for u in range(2):
-                t = 2 * f + u
                 dst = []
-                for d in range(16):
-                    if d == ch:
+                for it in PLAN:
+                    if it["pos"] < 0 or min(it["n"], 2) != i:
                         continue
-                    b = block_order(d).index(ch)
-                    c, slot, idx = landing(d, b, t)
-                    if idx == i:
-                        dst.append((b, c, slot))
+                    for j, (b, t) in enumerate(it["units"]):
+                        if t == 2 * f + u:
+                            d = [d for d in range(16) if d != ch and block_order(d)[b] == ch][0]
+                            dst.append((b, helper_list(d)[it["pos"]], it["slot"] + j))
                 dst.sort()
                 if dst:
                     trs.append(RemoteDMATransfer(dst_ids=[did(topo, c) for _, c, _ in dst],
@@ -126,17 +165,19 @@ def helper_core(g, core, T, topo):
             g.remote_dma_fused(trs, local_sem=sem.loc)
             loc += 4 * len(trs)
     r = did(topo, rcore(ch))
-    for i in range(3):
-        k = 1 + pos + 7 * i
-        if k >= NITEMS:
-            break
-        grp = (k + 2) % W
-        g.wait_ge(sem["h%d" % i], 12)
-        g.wait_ge(sem["c%d" % i], 1)
-        trs = [RemoteDMATransfer(dst_ids=[r], dma_engine_mask=0xF << (4 * j), remote_sem=sem["r%d" % grp],
-                                 src=buf[G * i + j], dst=buf[G * grp + j]) for j in range(G)]
+    mine = [it for it in PLAN if it["pos"] == pos]
+    for it in mine:
+        cls = min(it["n"], 2)
+        n = len(it["units"])
+        g.wait_ge(sem["h%d" % cls], 4 * sum(len(o["units"]) for o in mine if min(o["n"], 2) == cls))
+        if it["credit"]:
+            g.wait_ge(sem["c%d" % it["n"]], 1)
+        e = ENG[n]
+        trs = [RemoteDMATransfer(dst_ids=[r], dma_engine_mask=((1 << e) - 1) << (e * j),
+                                 remote_sem=sem["r%d" % it["grp"]], src=buf[it["slot"] + j],
+                                 dst=buf[GROUPS[it["grp"]][0] + j]) for j in range(n)]
         g.remote_dma_fused(trs, local_sem=sem.loc)
-        loc += 12
+        loc += e * n
     g.wait_ge(sem.loc, loc)
 
 

@@ -1,14 +1,16 @@
 from concourse.bass import DstId, RemoteDMATransfer
 
 NS, Q = 9, 4
-GROUPS = ((0, 2), (2, 2), (4, 2), (6, 2), (8, 1))
+GROUPS = tuple((s, 1) for s in range(NS))
+CL = (0, 1, 1, 2, 2, 2, 3, 3, 3)
+NCL = 4
 W = len(GROUPS)
-NC = 6
+NC = 9
 ENG = {1: 16, 2: 8, 3: 4, 4: 4, 5: 2}
 SCRATCH = {
     "buf": ("dram", [NS, 128, 32], "float32"),
 }
-SEMAPHORES = (["xld", "xl", "xs", "own", "loc", "h0", "h1", "h2"] + ["c%d" % i for i in range(NC)]
+SEMAPHORES = (["xld", "xl", "xs", "own", "loc"] + ["h%d" % i for i in range(NCL)] + ["c%d" % i for i in range(NC)]
               + ["r%d" % i for i in range(W)] + ["s%d" % i for i in range(W)])
 FC = (3, 6)
 STAGE = 7
@@ -48,8 +50,7 @@ def make_plan():
     while ptr < len(units):
         gi = min(range(W), key=lambda i: (nxt[i], i))
         take = min(GROUPS[gi][1], len(units) - ptr)
-        p = min([p for p in range(7) if free[p] - used[p] >= take],
-                key=lambda p: ((free[p] - used[p] - take) % 2 if take == 1 else 0, last[p]))
+        p = min([p for p in range(7) if free[p] - used[p] >= take], key=lambda p: last[p])
         items.append({"grp": gi, "units": units[ptr:ptr + take], "pos": p, "credit": not virgin[gi],
                       "n": count[p], "slot": used[p]})
         virgin[gi] = False
@@ -146,15 +147,15 @@ def helper_core(g, core, T, topo):
     if core % 8 in FC:
         f = FC.index(core % 8)
         g.wait_ge(sem.xs, 4)
-        for i in range(3):
+        for i in range(NCL):
             trs = []
             for u in range(2):
                 dst = []
                 for it in PLAN:
-                    if it["pos"] < 0 or min(it["n"], 2) != i:
+                    if it["pos"] < 0:
                         continue
                     for j, (b, t) in enumerate(it["units"]):
-                        if t == 2 * f + u:
+                        if t == 2 * f + u and CL[it["slot"] + j] == i:
                             d = [d for d in range(16) if d != ch and block_order(d)[b] == ch][0]
                             dst.append((b, helper_list(d)[it["pos"]], it["slot"] + j))
                 dst.sort()
@@ -162,14 +163,16 @@ def helper_core(g, core, T, topo):
                     trs.append(RemoteDMATransfer(dst_ids=[did(topo, c) for _, c, _ in dst],
                                                  dma_engine_mask=0xF << (4 * u), remote_sem=sem["h%d" % i],
                                                  srcs=[buf[STAGE + u]], dsts=[buf[slot] for _, _, slot in dst]))
-            g.remote_dma_fused(trs, local_sem=sem.loc)
-            loc += 4 * len(trs)
+            if trs:
+                g.remote_dma_fused(trs, local_sem=sem.loc)
+                loc += 4 * len(trs)
     r = did(topo, rcore(ch))
     mine = [it for it in PLAN if it["pos"] == pos]
+    filled = sum(len(it["units"]) for it in mine)
     for it in mine:
-        cls = min(it["n"], 2)
         n = len(it["units"])
-        g.wait_ge(sem["h%d" % cls], 4 * sum(len(o["units"]) for o in mine if min(o["n"], 2) == cls))
+        for cls in sorted(set(CL[it["slot"] + j] for j in range(n))):
+            g.wait_ge(sem["h%d" % cls], 4 * sum(1 for s in range(filled) if CL[s] == cls))
         if it["credit"]:
             g.wait_ge(sem["c%d" % it["n"]], 1)
         e = ENG[n]

from concourse.bass import DstId, RemoteDMATransfer

NS, Q = 9, 4
GROUPS = tuple((s, 1) for s in range(NS))
CL = (0, 1, 1, 2, 2, 2, 3, 3, 3)
NCL = 4
W = len(GROUPS)
NC = 9
ENG = {1: 16, 2: 8, 3: 4, 4: 4, 5: 2}
SCRATCH = {
    "buf": ("dram", [NS, 128, 32], "float32"),
}
SEMAPHORES = (["xld", "xl", "xs", "own", "loc"] + ["h%d" % i for i in range(NCL)] + ["c%d" % i for i in range(NC)]
              + ["r%d" % i for i in range(W)] + ["s%d" % i for i in range(W)])
FC = (3, 6)
STAGE = 7


def rcore(ch):
    return 8 * ch + (2 if ch % 2 == 0 else 5)


def helper_list(ch):
    r = rcore(ch) % 8
    return [8 * ch + k for k in range(8) if k != r and k not in FC] + [8 * ch + k for k in FC]


def block_order(d):
    return ([(d - 2) % 16, d ^ 1] + [(d - 2 * e) % 16 for e in range(2, 8)]
            + [((d ^ 1) - 2 * e) % 16 for e in range(1, 8)])


def make_plan():
    units = [(b, t) for b in range(15) for t in range(Q)]
    items, nxt, virgin, ptr = [], [], [], 0
    for gi, (s0, n) in enumerate(GROUPS):
        if s0 >= Q and ptr < Q:
            take = min(n, Q - ptr)
            items.append({"grp": gi, "units": units[ptr:ptr + take], "pos": -1, "credit": False})
            ptr += take
            nxt.append(5)
            virgin.append(False)
        else:
            nxt.append(4)
            virgin.append(s0 >= Q)
    free = [NS] * 5 + [STAGE] * 2
    used = [0] * 7
    count = [0] * 7
    last = [p - 7 for p in range(7)]
    while ptr < len(units):
        gi = min(range(W), key=lambda i: (nxt[i], i))
        take = min(GROUPS[gi][1], len(units) - ptr)
        p = min([p for p in range(7) if free[p] - used[p] >= take], key=lambda p: last[p])
        items.append({"grp": gi, "units": units[ptr:ptr + take], "pos": p, "credit": not virgin[gi],
                      "n": count[p], "slot": used[p]})
        virgin[gi] = False
        last[p] = len(items)
        used[p] += take
        count[p] += 1
        ptr += take
        nxt[gi] += 3
    return items


PLAN = make_plan()


def did(topo, c):
    rid, pid, _ = topo.addr(c)
    return DstId(rid=rid, pnc=pid)


def rank_core(g, core, T, topo):
    ch = core // 8
    sem, buf = T.sem, T.buf
    me = T.rank_of(core)
    g.sync.dma_start(buf[0:Q], T.x[:, :]).then_inc(sem.xld, 16)
    g.wait_ge(sem.xld, 16)
    trs = []
    for t in range(Q):
        trs.append(RemoteDMATransfer(dst_ids=[did(topo, 8 * ch + FC[t // 2])], dma_engine_mask=0x3 << (8 + 2 * t),
                                     remote_sem=sem.xs, src=buf[t], dst=buf[STAGE + t % 2]))
    nxt = did(topo, rcore((ch + 2) % 16))
    for it in PLAN:
        if it["pos"] < 0:
            for j, (b, t) in enumerate(it["units"]):
                trs.append(RemoteDMATransfer(dst_ids=[nxt], dma_engine_mask=0x3 << (2 * t),
                                             remote_sem=sem["r%d" % it["grp"]], src=buf[t],
                                             dst=buf[GROUPS[it["grp"]][0] + j]))
    g.remote_dma_fused(trs, local_sem=sem.xl)
    left = 2 * len(trs)
    g.scalar.wait_ge(sem.xl, left)
    g.scalar.dma_start(T.y[:, 128 * me:128 * me + 128], T.x[:, :]).then_inc(sem.own, 16)

    order = block_order(ch)
    hl = helper_list(ch)
    ncred = [0]

    def credit(it):
        rid, pid, _ = topo.addr(hl[it["pos"]])
        g.remote_sem_update(remote_sem=sem["c%d" % it["n"]], local_sem=sem.loc, pid=pid, routing_id=rid,
                            dma_engine_mask=1)
        ncred[0] += 1

    g.wait_ge(sem.xl, left)
    seen = set()
    for it in PLAN:
        if it["grp"] not in seen and it["credit"]:
            credit(it)
        seen.add(it["grp"])
    arrived = [0] * W
    stored = [0] * W
    queues = (g.sync, g.scalar)
    nq = 0
    for k, it in enumerate(PLAN):
        grp = it["grp"]
        n = len(it["units"])
        arrived[grp] += n * (2 if it["pos"] < 0 else ENG[n])
        runs = []
        for j, (b, t) in enumerate(it["units"]):
            if runs and runs[-1][0] == b:
                runs[-1][3] += 1
            else:
                runs.append([b, t, GROUPS[grp][0] + j, 1])
        for b, t, slot, m in runs:
            q = queues[nq % 2]
            nq += 1
            col = 128 * T.rank_of(rcore(order[b]))
            q.wait_ge(sem["r%d" % grp], arrived[grp])
            q.dma_start(T.y[32 * t:32 * (t + m), col:col + 128],
                        buf[slot:slot + m]).then_inc(sem["s%d" % grp], 16)
            stored[grp] += 16
        g.wait_ge(sem["s%d" % grp], stored[grp])
        for later in PLAN[k + 1:]:
            if later["grp"] == grp:
                credit(later)
                break
    g.wait_ge(sem.own, 16)
    g.wait_ge(sem.loc, ncred[0])


def helper_core(g, core, T, topo):
    ch = core // 8
    sem, buf = T.sem, T.buf
    pos = helper_list(ch).index(core)
    loc = 0
    if core % 8 in FC:
        f = FC.index(core % 8)
        g.wait_ge(sem.xs, 4)
        for i in range(NCL):
            trs = []
            for u in range(2):
                dst = []
                for it in PLAN:
                    if it["pos"] < 0:
                        continue
                    for j, (b, t) in enumerate(it["units"]):
                        if t == 2 * f + u and CL[it["slot"] + j] == i:
                            d = [d for d in range(16) if d != ch and block_order(d)[b] == ch][0]
                            dst.append((b, helper_list(d)[it["pos"]], it["slot"] + j))
                dst.sort()
                if dst:
                    trs.append(RemoteDMATransfer(dst_ids=[did(topo, c) for _, c, _ in dst],
                                                 dma_engine_mask=0xF << (4 * u), remote_sem=sem["h%d" % i],
                                                 srcs=[buf[STAGE + u]], dsts=[buf[slot] for _, _, slot in dst]))
            if trs:
                g.remote_dma_fused(trs, local_sem=sem.loc)
                loc += 4 * len(trs)
    r = did(topo, rcore(ch))
    mine = [it for it in PLAN if it["pos"] == pos]
    filled = sum(len(it["units"]) for it in mine)
    for it in mine:
        n = len(it["units"])
        for cls in sorted(set(CL[it["slot"] + j] for j in range(n))):
            g.wait_ge(sem["h%d" % cls], 4 * sum(1 for s in range(filled) if CL[s] == cls))
        if it["credit"]:
            g.wait_ge(sem["c%d" % it["n"]], 1)
        e = ENG[n]
        trs = [RemoteDMATransfer(dst_ids=[r], dma_engine_mask=((1 << e) - 1) << (e * j),
                                 remote_sem=sem["r%d" % it["grp"]], src=buf[it["slot"] + j],
                                 dst=buf[GROUPS[it["grp"]][0] + j]) for j in range(n)]
        g.remote_dma_fused(trs, local_sem=sem.loc)
        loc += e * n
    g.wait_ge(sem.loc, loc)


def rank_program(g, core, T, topo):
    if core == rcore(core // 8):
        rank_core(g, core, T, topo)
    else:
        helper_core(g, core, T, topo)
